import numpy as np
import ml_dtypes


def mxq(x, axis, fmt="e4m3"):
    dtype, down = {"e4m3": (ml_dtypes.float8_e4m3fn, 7), "e5m2": (ml_dtypes.float8_e5m2, 14)}[fmt]
    v = np.moveaxis(np.asarray(x, np.float32).astype(ml_dtypes.bfloat16).astype(np.float64), axis, -1)
    blocks = v.reshape(v.shape[:-1] + (-1, 32))
    amax = np.abs(blocks).max(-1, keepdims=True)
    byte = np.maximum(np.where(amax > 0, np.frexp(amax)[1] - 1 + 127, 0) - down, 1)
    scale = np.exp2(byte - 127.0)
    codes = (blocks / scale).astype(np.float32).astype(dtype).astype(np.float64)
    return np.moveaxis((codes * scale).reshape(v.shape), -1, axis)


WIDE = False


def mx_kscale(k):
    if not WIDE:
        return np.ones(k)
    levels = np.array([10, -10, 5, -5, 0])
    if k % 512:
        return np.exp2(np.random.permutation(np.resize(levels, k // 32))).repeat(32)
    a = np.empty((k // 512, 16))
    for p in range(k // 512):
        a[p, :8] = np.random.permutation(np.resize(levels, 8))
        for g in range(8):
            far = levels[np.abs(levels - a[p, g]) >= 10]
            a[p, g + 8] = far[np.random.randint(len(far))]
    return np.exp2(a.ravel()).repeat(32)


BF16 = ml_dtypes.bfloat16


def bf(x):
    return np.asarray(x, np.float32).astype(BF16)


def f64(x):
    return np.asarray(x).astype(np.float64)


S, M, D, E, G = 4096, 512, 512, 2, 64
U = D // G


def softmax(z, axis):
    e = np.exp(z - z.max(axis=axis, keepdims=True))
    return e / e.sum(axis=axis, keepdims=True)


def draw0():
    s, t = mx_kscale(D), mx_kscale(M)
    return {
        "x": bf(np.random.standard_normal((S, D))),
        "a": bf(np.random.standard_normal((E, D)) * 1.6 * s[None, :]),
        "k": bf(np.random.standard_normal((M, D)) / s[None, :]),
        "u": bf(np.random.standard_normal((E, M)) * 0.25 * np.sqrt(M) * t[None, :]),
        "v": bf(np.random.standard_normal((M, D)) / t[:, None]),
        "wg": bf(np.random.standard_normal((D, E, G)) * 1.5 / np.sqrt(D)),
        "bg": bf(np.random.standard_normal((E, G)) * 0.5),
    }


def expert_attention(x, a, k, u, v):
    q = f64(x)[None, :, :] * f64(a)[:, None, :]
    kq = mxq(f64(k), 1, "e4m3")
    scores = (mxq(q, 2, "e4m3") @ kq.T) / np.sqrt(D)
    p = softmax(scores, -1)
    pu = p * f64(u)[:, None, :]
    return mxq(pu, 2, "e4m3") @ mxq(f64(v), 0, "e4m3")


def group_gates(x, wg, bg):
    logits = f64(x) @ f64(wg).reshape(D, E * G)
    logits = logits.reshape(S, E, G) + f64(bg)[None, :, :]
    return softmax(logits, 1)


def core(x, a, k, u, v, wg, bg):
    o = expert_attention(x, a, k, u, v)
    g = group_gates(x, wg, bg)
    g_full = np.repeat(g, U, axis=-1)
    return np.sum(g_full.transpose(1, 0, 2) * o, axis=0)


def e4m3fn_bytes(y):
    return np.clip(np.asarray(y, np.float64), -448.0, 448.0).astype(np.float32).astype(ml_dtypes.float8_e4m3fn).view(np.uint8)


def e4m3fn_values(b):
    return np.asarray(b, np.uint8).view(ml_dtypes.float8_e4m3fn).astype(np.float64)


def setup_inputs():
    d = draw0()
    x0 = np.asarray(d['v']).astype(np.float64)
    s = (np.max(np.abs(x0), axis=(1,), keepdims=True) / 448.0).astype(np.float32)
    out = {}
    for k, v in d.items():
        if k == 'v':
            out['v_bytes'] = e4m3fn_bytes(x0 / s.astype(np.float64))
            out['v_scale'] = s
        else:
            out[k] = v
    return out


def reference(x, a, k, u, v_bytes, v_scale, wg, bg):
    return core(x, a, k, u, e4m3fn_values(v_bytes) * v_scale.astype(np.float64), wg, bg)

@@ -1,0 +1,235 @@
+from contextlib import ExitStack
+
+import concourse.mybir as mybir
+from concourse.masks import make_identity
+
+S, D, M, E, G = 4096, 512, 512, 2, 64
+FLOPS = 2 * S * (2 * E * D * M + D * E * G)
+
+F32 = mybir.dt.float32
+BF16 = mybir.dt.bfloat16
+U32 = mybir.dt.uint32
+U8 = mybir.dt.uint8
+X4 = mybir.dt.float8_e4m3fn_x4
+FP8 = mybir.dt.float8_e4m3fn
+ALU = mybir.AluOpType
+ACT = mybir.ActivationFunctionType
+AX = mybir.AxisListType
+
+P = 128
+NT = S // P
+TB = 4
+NB = NT // TB
+SCALE = 1.0 / float(D) ** 0.5
+
+
+def tile_mixtureofattentionheadssharedkv_t_kernel(tc, x, a, k, u, v_bytes, v_scale, wg, bg, out):
+    nc = tc.nc
+    with ExitStack() as ctx:
+        keep = ctx.enter_context(tc.tile_pool(name="keep", bufs=1))
+        work = ctx.enter_context(tc.tile_pool(name="work", bufs=4))
+        psum = ctx.enter_context(tc.psum_pool(name="psum", bufs=1))
+        ctx.enter_context(tc.manual_schedule())
+
+        sc = [psum.tile([P, M], F32, name="sc0"), psum.tile([P, M], F32, name="sc1")]
+        ub = [psum.tile([P, M], F32, name="ub0"), psum.tile([P, M], F32, name="ub1")]
+        pt = psum.tile([P, M], F32, name="pt")
+        od = psum.tile([P, D], F32, name="od")
+        o1 = psum.tile([P, D], F32, name="o1")
+        xz = psum.tile([P, M], F32, name="xz")
+
+        k_sb = keep.tile([P, 4, D], BF16, name="k_sb")
+        aT = keep.tile([P, E, 4], BF16, name="aT")
+        w_sb = keep.tile([P, 4, E, G], BF16, name="w_sb")
+        wn = keep.tile([P, 4, G], BF16, name="wn")
+        ue = keep.tile([P, E, M], BF16, name="ue")
+        up = keep.tile([P, E, M], BF16, name="up")
+        sgn = keep.tile([P, P], BF16, name="sgn")
+        brow = keep.tile([P, G], BF16, name="brow")
+        ident = keep.tile([P, P], F32, name="ident")
+        vb = keep.tile([P, 4, D], U8, name="vb")
+        vs = keep.tile([P, 4], F32, name="vs")
+        vpl = keep.tile([P, 4, D], BF16, name="vpl", align_bytes=64)
+        vil = keep.tile([P, D, 4], BF16, name="vil", align_bytes=64)
+        vc = keep.tile([P, D], U32, name="vc", align_bytes=64)
+        vq = keep.tile([P, D], U8, name="vq", align_bytes=64)
+        kil = keep.tile([P, M * 4], BF16, name="kil", align_bytes=64)
+        kc = keep.tile([P, M], U32, name="kc", align_bytes=64)
+        kq = keep.tile([P, M], U8, name="kq", align_bytes=64)
+        warm = keep.tile([P, 1], F32, name="warm")
+
+        x_blocks = x.rearrange("(b p j) d -> b p j d", p=P, j=TB)
+        out_blocks = out.rearrange("(b p j) d -> b p j d", p=P, j=TB)
+        xb = [keep.tile([P, TB, D], BF16, name="xb%d" % b) for b in range(NB)]
+
+        k_rows = k.rearrange("(p j) d -> p j d", j=4)
+        nc.sync.dma_start(out=k_sb[:, 0:2, :], in_=k_rows[:, 0:2, :])
+        nc.sync.dma_start(out=k_sb[:, 2:4, :], in_=k_rows[:, 2:4, :])
+        nc.sync.dma_start(out=xb[0][:], in_=x_blocks[0])
+        nc.sync.dma_start(out=w_sb[:], in_=wg.rearrange("(p t) e j -> p t e j", t=4))
+        nc.sync.dma_start(out=vb[:], in_=v_bytes.rearrange("(p t) d -> p t d", t=4))
+        nc.sync.dma_start(out=xb[1][:], in_=x_blocks[1])
+
+        nc.vector.memset(warm[:], 0.0)
+        nc.vector.memset(ue[:], 0.0)
+        make_identity(nc, ident[:])
+        nc.gpsimd.memset(brow[:], 0.0)
+        nc.gpsimd.memset(sgn[:], -1.0)
+        nc.gpsimd.memset(sgn[0:32, :], 1.0)
+        nc.scalar.activation(out=warm[:], in_=warm[:], func=ACT.Exp)
+        nc.scalar.dma_start(out=aT[:], in_=a.rearrange("e (p t) -> p e t", t=4))
+        nc.scalar.dma_start(out=ue[0:1, 0, :], in_=u[0:1, :])
+        nc.scalar.dma_start(out=ue[32:33, 1, :], in_=u[1:2, :])
+        nc.scalar.dma_start(out=brow[0:1, :], in_=bg[0:1, :])
+        nc.scalar.dma_start(out=brow[32:33, :], in_=bg[1:2, :])
+        nc.scalar.dma_start(out=vs[:], in_=v_scale.rearrange("(p t) o -> p (t o)", t=4))
+
+        for j in range(4):
+            words = k_sb[:, j, :].bitcast(F32)
+            for h in range(2):
+                col = ((j % 2) * 2 + h) * P
+                nc.tensor.transpose(sc[j // 2][:, col:col + P], words[:, h::2], ident[:])
+        kw = kil[:].bitcast(F32).rearrange("p (u r c h) -> p u r c h", u=2, c=2, h=2)
+        nc.vector.tensor_copy(out=kw[:, 0], in_=sc[0][:].rearrange("p (c h r) -> p r c h", c=2, h=2))
+        nc.scalar.copy(out=kw[:, 1], in_=sc[1][:].rearrange("p (c h r) -> p r c h", c=2, h=2))
+        nc.vector.tensor_copy(
+            out=up[:].rearrange("p e (h q c) -> p (e h) q c", h=2, c=2)[:, 0:2],
+            in_=ue[:, 0, :].rearrange("p (q h c) -> p h q c", h=2, c=2))
+        nc.vector.tensor_copy(
+            out=up[:].rearrange("p e (h q c) -> p (e h) q c", h=2, c=2)[:, 2:4],
+            in_=ue[:, 1, :].rearrange("p (q h c) -> p h q c", h=2, c=2))
+        nc.vector.quantize_mx(out=kc[:].bitcast(X4), scales=kq[:], in_=kil[:])
+        nc.vector.tensor_scalar(out=wn[:], in0=w_sb[:, :, 1, :], scalar1=-1.0, scalar2=None, op0=ALU.mult)
+        for b in range(2, NB):
+            nc.sync.dma_start(out=xb[b][:], in_=x_blocks[b])
+
+        st = {}
+
+        def buf(name, i, shape, dtype, bufs, align=32):
+            if (name, i) not in st:
+                st[name, i] = work.tile(shape, dtype, name=name, bufs=bufs, align_bytes=align)
+            return st[name, i]
+
+        def x_transpose(i):
+            words = xb[i // TB][:, i % TB, :].bitcast(F32)
+            for h in range(2):
+                nc.tensor.transpose(xz[:, h * P:(h + 1) * P], words[:, h::2], ident[:])
+
+        def x_copy(i):
+            nc.scalar.copy(out=buf("xts", i, [P, 2 * P], F32, 4, 64)[:], in_=xz[:, 0:2 * P])
+
+        def q_mult(i, e):
+            qb = buf("qb", i, [P, E, P, 4], BF16, 2, 64)
+            nc.vector.tensor_tensor(
+                out=qb[:, e].rearrange("p r (h c) -> p r h c", c=2),
+                in0=xz[:, 0:2 * P].bitcast(BF16).rearrange("p (h r c) -> p r h c", h=2, c=2),
+                in1=aT[:, e, :].rearrange("p (h c) -> p h c", c=2).unsqueeze(1).to_broadcast([P, P, 2, 2]),
+                op=ALU.mult)
+
+        def q_quant(i):
+            nc.vector.quantize_mx(out=buf("qc", i, [P, E * P], U32, 4, 64)[:].bitcast(X4),
+                                  scales=buf("qs", i, [P, E * P], U8, 4, 64)[:],
+                                  in_=st["qb", i][:].rearrange("p e r t -> p (e r t)"))
+
+        def gates(i):
+            z = xz[:, 2 * P + (i % 4) * G:2 * P + (i % 4 + 1) * G]
+            xt = st["xts", i][:].bitcast(BF16).rearrange("p (h r c) -> p h c r", h=2, c=2)
+            nc.tensor.matmul(z, lhsT=sgn[:], rhs=brow[:], start=True, stop=False)
+            for t in range(4):
+                nc.tensor.matmul(z, lhsT=xt[:, t // 2, t % 2, :], rhs=w_sb[:, t, 0, :], start=False, stop=False)
+                nc.tensor.matmul(z, lhsT=xt[:, t // 2, t % 2, :], rhs=wn[:, t, :], start=False, stop=(t == 3))
+
+        def gate_act(i):
+            if i % 2 == 1:
+                z = xz[:, 2 * P + (i % 4 - 1) * G:2 * P + (i % 4 + 1) * G]
+                th = buf("th", i // 2, [P, 2 * G], F32, 3)
+                nc.scalar.activation(out=th[:], in_=z, func=ACT.Tanh, scale=0.5)
+                nc.scalar.activation(out=buf("g", i // 2, [P, 2, G], F32, 4)[:].rearrange("p i j -> p (i j)"),
+                                     in_=th[:], func=ACT.Copy, scale=0.5, bias=0.5)
+
+        def score(i, e):
+            cols = slice(e * P, (e + 1) * P)
+            nc.tensor.matmul_mx(out=sc[e][:], lhsT=st["qc", i][:, cols].bitcast(X4), lhsT_scale=st["qs", i][:, cols],
+                                rhs=kc[:].bitcast(X4), rhs_scale=kq[:], start=True, stop=True)
+
+        def row_max(i, e):
+            nc.vector.tensor_reduce(out=buf("mx%d" % e, i, [P, 1], F32, 4)[:], in_=sc[e][:], axis=AX.X, op=ALU.max)
+
+        def neg_max(i, e):
+            nc.scalar.activation(out=buf("nm%d" % e, i, [P, 1], F32, 4)[:], in_=st["mx%d" % e, i][:], func=ACT.Copy, scale=-SCALE)
+
+        def exp(i, e):
+            nc.scalar.activation(out=buf("ee%d" % e, i, [P, M], F32, 2)[:], in_=sc[e][:], func=ACT.Exp, scale=SCALE,
+                                 bias=st["nm%d" % e, i][:], accum_out=buf("rs", i, [P, E], F32, 4)[:, e:e + 1])
+
+        def recip(i):
+            nc.vector.reciprocal(buf("ri", i, [P, E], F32, 4)[:], st["rs", i][:])
+
+        def p_mult(i, e):
+            nc.vector.scalar_tensor_tensor(out=buf("pu%d" % e, i, [P, M], BF16, 2)[:], in0=st["ee%d" % e, i][:],
+                                           scalar=st["ri", i][:, e:e + 1], in1=ub[e][:], op0=ALU.mult, op1=ALU.mult)
+
+        def p_transpose(i, e):
+            words = st["pu%d" % e, i][:].bitcast(F32)
+            for h in range(2):
+                col = (e * 2 + h) * P
+                nc.tensor.transpose(pt[:, col:col + P], words[:, h * P:(h + 1) * P], ident[:])
+
+        def p_copy(i):
+            nc.scalar.copy(out=buf("pT", i, [P, E * P * 4], BF16, 2, 64)[:].bitcast(F32).rearrange("p (e r h) -> p e r h", e=E, h=2),
+                           in_=pt[:].rearrange("p (e h r) -> p e r h", e=E, h=2))
+
+        def p_quant(i):
+            nc.vector.quantize_mx(out=buf("pc", i, [P, E * P], U32, 2, 64)[:].bitcast(X4),
+                                  scales=buf("ps", i, [P, E * P], U8, 2, 64)[:], in_=st["pT", i][:])
+
+        def out_mm(i, dst, e, first, last):
+            cols = slice(e * P, (e + 1) * P)
+            nc.tensor.matmul_mx(out=dst[:], lhsT=st["pc", i][:, cols].bitcast(X4), lhsT_scale=st["ps", i][:, cols],
+                                rhs=vc[:].bitcast(X4), rhs_scale=vq[:], start=first, stop=last)
+
+        def out_diff(i):
+            out_mm(i, od, 0, True, False)
+            out_mm(i, od, 1, False, True)
+
+        def out_one(i):
+            out_mm(i, o1, 1, True, True)
+
+        def diff_copy(i):
+            nc.scalar.copy(out=buf("ds", i, [P, D], F32, 2)[:], in_=od[:])
+
+        def one_copy(i):
+            nc.scalar.copy(out=buf("oc", i, [P, D], F32, 2)[:], in_=o1[:])
+
+        def gate_mult(i):
+            nc.gpsimd.tensor_tensor(
+                out=buf("t", i, [P, D], F32, 3)[:].rearrange("p (j c) -> p j c", c=8),
+                in0=st["ds", i][:].rearrange("p (j c) -> p j c", c=8),
+                in1=st["g", i // 2][:, i % 2, :].unsqueeze(2).to_broadcast([P, G, 8]), op=ALU.mult)
+
+        def gate_sub(i):
+            r = buf("r", i, [P, D], F32, 4)
+            nc.gpsimd.tensor_tensor(out=r[:], in0=st["t", i][:], in1=st["oc", i][:], op=ALU.subtract)
+            nc.sync.dma_start(out=out_blocks[i // TB][:, i % TB, :], in_=r[:])
+
+        stages = {
+            "xT": (x_transpose,), "xc": (x_copy,), "qm0": (q_mult, 0), "qm1": (q_mult, 1), "qq": (q_quant,),
+            "gt": (gates,), "ga": (gate_act,), "sc0": (score, 0), "sc1": (score, 1), "mx0": (row_max, 0), "mx1": (row_max, 1),
+            "nm0": (neg_max, 0), "nm1": (neg_max, 1), "ex0": (exp, 0), "ex1": (exp, 1), "rc": (recip,),
+            "pm0": (p_mult, 0), "pm1": (p_mult, 1), "pt0": (p_transpose, 0), "pt1": (p_transpose, 1), "pc": (p_copy,), "pq": (p_quant,),
+            "oD": (out_diff,), "oO": (out_one,), "cD": (diff_copy,), "cO": (one_copy,), "gm": (gate_mult,), "gs": (gate_sub,),
+        }
+        order = [("rc", 3), ("nm1", 2), ("sc0", 2), ("cO", 6), ("gt", 3), ("pq", 5), ("qq", 1), ("mx0", 2), ("ex1", 2), ("nm0", 2), ("pt0", 4), ("pm1", 3), ("pc", 4), ("gm", 6), ("xT", 0), ("ex0", 2), ("oD", 5), ("qm1", 0), ("gs", 6), ("sc1", 1), ("qm0", 0), ("xc", 0), ("ga", 3), ("pt1", 3), ("cD", 5), ("pm0", 3), ("mx1", 1), ("oO", 5)]
+        for n in range(NT + max(lag for name, lag in order)):
+            for name, lag in order:
+                if 0 <= n - lag < NT:
+                    stages[name][0](n - lag, *stages[name][1:])
+            if n == 0:
+                for e in range(E):
+                    nc.tensor.matmul(ub[e][:], lhsT=sgn[:], rhs=up[:, e, :], start=True, stop=True)
+                for t in range(4):
+                    nc.scalar.activation(out=vpl[:, t, :], in_=vb[:, t, :].bitcast(FP8), func=ACT.Copy, scale=vs[:, t:t + 1])
+            if n == 1:
+                nc.vector.tensor_copy(out=vil[:], in_=vpl[:].rearrange("p t d -> p d t"))
+            if n == 2:
+                nc.vector.quantize_mx(out=vc[:].bitcast(X4), scales=vq[:], in_=vil[:].rearrange("p d t -> p (d t)"))

@@ -20,6 +20,7 @@ P = 128
 NT = S // P
 TB = 4
 NB = NT // TB
+TV = 4
 SCALE = 1.0 / float(D) ** 0.5
 
 
@@ -43,7 +44,6 @@ def tile_mixtureofattentionheadssharedkv_t_kernel(tc, x, a, k, u, v_bytes, v_sca
         w_sb = keep.tile([P, 4, E, G], BF16, name="w_sb")
         wn = keep.tile([P, 4, G], BF16, name="wn")
         ue = keep.tile([P, E, M], BF16, name="ue")
-        up = keep.tile([P, E, M], BF16, name="up")
         sgn = keep.tile([P, P], BF16, name="sgn")
         brow = keep.tile([P, G], BF16, name="brow")
         ident = keep.tile([P, P], F32, name="ident")
@@ -63,12 +63,14 @@ def tile_mixtureofattentionheadssharedkv_t_kernel(tc, x, a, k, u, v_bytes, v_sca
         xb = [keep.tile([P, TB, D], BF16, name="xb%d" % b) for b in range(NB)]
 
         k_rows = k.rearrange("(p j) d -> p j d", j=4)
+        nc.sync.dma_start(out=xb[0][:, 0:1, :], in_=x_blocks[0][:, 0:1, :])
         nc.sync.dma_start(out=k_sb[:, 0:2, :], in_=k_rows[:, 0:2, :])
         nc.sync.dma_start(out=k_sb[:, 2:4, :], in_=k_rows[:, 2:4, :])
-        nc.sync.dma_start(out=xb[0][:], in_=x_blocks[0])
-        nc.sync.dma_start(out=w_sb[:], in_=wg.rearrange("(p t) e j -> p t e j", t=4))
+        nc.sync.dma_start(out=xb[0][:, 1:4, :], in_=x_blocks[0][:, 1:4, :])
         nc.sync.dma_start(out=vb[:], in_=v_bytes.rearrange("(p t) d -> p t d", t=4))
-        nc.sync.dma_start(out=xb[1][:], in_=x_blocks[1])
+        nc.sync.dma_start(out=w_sb[:], in_=wg.rearrange("(p t) e j -> p t e j", t=4))
+        for b in range(1, NB):
+            nc.sync.dma_start(out=xb[b][:], in_=x_blocks[b])
 
         nc.vector.memset(warm[:], 0.0)
         nc.vector.memset(ue[:], 0.0)
@@ -84,24 +86,33 @@ def tile_mixtureofattentionheadssharedkv_t_kernel(tc, x, a, k, u, v_bytes, v_sca
         nc.scalar.dma_start(out=brow[32:33, :], in_=bg[1:2, :])
         nc.scalar.dma_start(out=vs[:], in_=v_scale.rearrange("(p t) o -> p (t o)", t=4))
 
-        for j in range(4):
-            words = k_sb[:, j, :].bitcast(F32)
+        nc.gpsimd.tensor_scalar(out=wn[:], in0=w_sb[:, :, 1, :], scalar1=-1.0, scalar2=0.0, op0=ALU.mult, op1=ALU.add)
+
+        def k_transpose():
+            for j in range(4):
+                words = k_sb[:, j, :].bitcast(F32)
+                for h in range(2):
+                    col = ((j % 2) * 2 + h) * P
+                    nc.tensor.transpose(sc[j // 2][:, col:col + P], words[:, h::2], ident[:])
+            kw = kil[:].bitcast(F32).rearrange("p (u r c h) -> p u r c h", u=2, c=2, h=2)
+            nc.vector.tensor_copy(out=kw[:, 0], in_=sc[0][:].rearrange("p (c h r) -> p r c h", c=2, h=2))
+            nc.scalar.copy(out=kw[:, 1], in_=sc[1][:].rearrange("p (c h r) -> p r c h", c=2, h=2))
+
+        def k_quant():
             for h in range(2):
-                col = ((j % 2) * 2 + h) * P
-                nc.tensor.transpose(sc[j // 2][:, col:col + P], words[:, h::2], ident[:])
-        kw = kil[:].bitcast(F32).rearrange("p (u r c h) -> p u r c h", u=2, c=2, h=2)
-        nc.vector.tensor_copy(out=kw[:, 0], in_=sc[0][:].rearrange("p (c h r) -> p r c h", c=2, h=2))
-        nc.scalar.copy(out=kw[:, 1], in_=sc[1][:].rearrange("p (c h r) -> p r c h", c=2, h=2))
-        nc.vector.tensor_copy(
-            out=up[:].rearrange("p e (h q c) -> p (e h) q c", h=2, c=2)[:, 0:2],
-            in_=ue[:, 0, :].rearrange("p (q h c) -> p h q c", h=2, c=2))
-        nc.vector.tensor_copy(
-            out=up[:].rearrange("p e (h q c) -> p (e h) q c", h=2, c=2)[:, 2:4],
-            in_=ue[:, 1, :].rearrange("p (q h c) -> p h q c", h=2, c=2))
-        nc.vector.quantize_mx(out=kc[:].bitcast(X4), scales=kq[:], in_=kil[:])
-        nc.vector.tensor_scalar(out=wn[:], in0=w_sb[:, :, 1, :], scalar1=-1.0, scalar2=None, op0=ALU.mult)
-        for b in range(2, NB):
-            nc.sync.dma_start(out=xb[b][:], in_=x_blocks[b])
+                nc.vector.quantize_mx(out=kc[:, h * 256:(h + 1) * 256].bitcast(X4), scales=kq[:, h * 256:(h + 1) * 256],
+                                      in_=kil[:, h * 1024:(h + 1) * 1024])
+
+        def v_widen():
+            for e in range(E):
+                nc.tensor.matmul(ub[e][:].rearrange("p (h q c) -> p h q c", h=2, c=2), lhsT=sgn[:],
+                                 rhs=ue[:, e, :].rearrange("p (q h c) -> p h q c", h=2, c=2), start=True, stop=True)
+            for t in range(4):
+                nc.scalar.activation(out=vpl[:, t, :], in_=vb[:, t, :].bitcast(FP8), func=ACT.Copy, scale=vs[:, t:t + 1])
+            nc.gpsimd.tensor_scalar(out=vil[:], in0=vpl[:].rearrange("p t d -> p d t"), scalar1=1.0, scalar2=0.0, op0=ALU.mult, op1=ALU.add)
+
+        def v_quant():
+            nc.vector.quantize_mx(out=vc[:].bitcast(X4), scales=vq[:], in_=vil[:].rearrange("p d t -> p (d t)"))
 
         st = {}
 
@@ -196,20 +207,26 @@ def tile_mixtureofattentionheadssharedkv_t_kernel(tc, x, a, k, u, v_bytes, v_sca
             out_mm(i, o1, 1, True, True)
 
         def diff_copy(i):
-            nc.scalar.copy(out=buf("ds", i, [P, D], F32, 2)[:], in_=od[:])
+            if i < NT - TV:
+                nc.scalar.copy(out=buf("ds", i, [P, D], F32, 2)[:], in_=od[:])
 
         def one_copy(i):
-            nc.scalar.copy(out=buf("oc", i, [P, D], F32, 2)[:], in_=o1[:])
+            if i < NT - TV:
+                nc.scalar.copy(out=buf("oc", i, [P, D], F32, 2)[:], in_=o1[:])
 
         def gate_mult(i):
-            nc.gpsimd.tensor_tensor(
+            tail = i >= NT - TV
+            eng = nc.vector if tail else nc.gpsimd
+            eng.tensor_tensor(
                 out=buf("t", i, [P, D], F32, 3)[:].rearrange("p (j c) -> p j c", c=8),
-                in0=st["ds", i][:].rearrange("p (j c) -> p j c", c=8),
+                in0=(od if tail else st["ds", i])[:].rearrange("p (j c) -> p j c", c=8),
                 in1=st["g", i // 2][:, i % 2, :].unsqueeze(2).to_broadcast([P, G, 8]), op=ALU.mult)
 
         def gate_sub(i):
             r = buf("r", i, [P, D], F32, 4)
-            nc.gpsimd.tensor_tensor(out=r[:], in0=st["t", i][:], in1=st["oc", i][:], op=ALU.subtract)
+            tail = i >= NT - TV
+            eng = nc.vector if tail else nc.gpsimd
+            eng.tensor_tensor(out=r[:], in0=st["t", i][:], in1=(o1 if tail else st["oc", i])[:], op=ALU.subtract)
             nc.sync.dma_start(out=out_blocks[i // TB][:, i % TB, :], in_=r[:])
 
         stages = {
@@ -219,17 +236,11 @@ def tile_mixtureofattentionheadssharedkv_t_kernel(tc, x, a, k, u, v_bytes, v_sca
             "pm0": (p_mult, 0), "pm1": (p_mult, 1), "pt0": (p_transpose, 0), "pt1": (p_transpose, 1), "pc": (p_copy,), "pq": (p_quant,),
             "oD": (out_diff,), "oO": (out_one,), "cD": (diff_copy,), "cO": (one_copy,), "gm": (gate_mult,), "gs": (gate_sub,),
         }
-        order = [("rc", 3), ("nm1", 2), ("sc0", 2), ("cO", 6), ("gt", 3), ("pq", 5), ("qq", 1), ("mx0", 2), ("ex1", 2), ("nm0", 2), ("pt0", 4), ("pm1", 3), ("pc", 4), ("gm", 6), ("xT", 0), ("ex0", 2), ("oD", 5), ("qm1", 0), ("gs", 6), ("sc1", 1), ("qm0", 0), ("xc", 0), ("ga", 3), ("pt1", 3), ("cD", 5), ("pm0", 3), ("mx1", 1), ("oO", 5)]
+        order = [("pt1", 5), ("ex0", 4), ("mx1", 3), ("pm0", 5), ("xc", 1), ("oO", 7), ("sc0", 3), ("rc", 4), ("qq", 2), ("ga", 6), ("pq", 6), ("nm1", 3), ("mx0", 3), ("cD", 7), ("ex1", 3), ("gm", 7), ("cO", 7), ("gt", 4), ("pt0", 5), ("gs", 7), ("xT", 0), ("sc1", 2), ("pm1", 4), ("oD", 6), ("nm0", 3), ("pc", 5), ("qm1", 0), ("qm0", 0)]
+        prologue = {0: k_transpose, 1: k_quant, 2: v_widen, 4: v_quant}
         for n in range(NT + max(lag for name, lag in order)):
             for name, lag in order:
                 if 0 <= n - lag < NT:
                     stages[name][0](n - lag, *stages[name][1:])
-            if n == 0:
-                for e in range(E):
-                    nc.tensor.matmul(ub[e][:], lhsT=sgn[:], rhs=up[:, e, :], start=True, stop=True)
-                for t in range(4):
-                    nc.scalar.activation(out=vpl[:, t, :], in_=vb[:, t, :].bitcast(FP8), func=ACT.Copy, scale=vs[:, t:t + 1])
-            if n == 1:
-                nc.vector.tensor_copy(out=vil[:], in_=vpl[:].rearrange("p t d -> p d t"))
-            if n == 2:
-                nc.vector.quantize_mx(out=vc[:].bitcast(X4), scales=vq[:], in_=vil[:].rearrange("p d t -> p (d t)"))
+            if n in prologue:
+                prologue[n]()

@@ -33,11 +33,13 @@ def tile_mixtureofattentionheadssharedkv_t_kernel(tc, x, a, k, u, v_bytes, v_sca
         ctx.enter_context(tc.manual_schedule())
 
         sc = [psum.tile([P, M], F32, name="sc0"), psum.tile([P, M], F32, name="sc1")]
-        ub = [psum.tile([P, M], F32, name="ub0"), psum.tile([P, M], F32, name="ub1")]
+        ub = psum.tile([P, E, M], BF16, name="ub")
         pt = psum.tile([P, M], F32, name="pt")
         od = psum.tile([P, D], F32, name="od")
         o1 = psum.tile([P, D], F32, name="o1")
-        xz = psum.tile([P, M], F32, name="xz")
+        xp = psum.tile([P, 2 * 2 * P], F32, name="xp")
+        zs = psum.tile([P, 8, G], F32, name="zs")
+        x_bank = {1: od, 2: o1}
 
         k_sb = keep.tile([P, 4, D], BF16, name="k_sb")
         aT = keep.tile([P, E, 4], BF16, name="aT")
@@ -63,10 +65,10 @@ def tile_mixtureofattentionheadssharedkv_t_kernel(tc, x, a, k, u, v_bytes, v_sca
         xb = [keep.tile([P, TB, D], BF16, name="xb%d" % b) for b in range(NB)]
 
         k_rows = k.rearrange("(p j) d -> p j d", j=4)
-        nc.sync.dma_start(out=xb[0][:, 0:1, :], in_=x_blocks[0][:, 0:1, :])
+        nc.sync.dma_start(out=xb[0][:, 0:2, :], in_=x_blocks[0][:, 0:2, :])
         nc.sync.dma_start(out=k_sb[:, 0:2, :], in_=k_rows[:, 0:2, :])
         nc.sync.dma_start(out=k_sb[:, 2:4, :], in_=k_rows[:, 2:4, :])
-        nc.sync.dma_start(out=xb[0][:, 1:4, :], in_=x_blocks[0][:, 1:4, :])
+        nc.sync.dma_start(out=xb[0][:, 2:4, :], in_=x_blocks[0][:, 2:4, :])
         nc.sync.dma_start(out=vb[:], in_=v_bytes.rearrange("(p t) d -> p t d", t=4))
         nc.sync.dma_start(out=w_sb[:], in_=wg.rearrange("(p t) e j -> p t e j", t=4))
         for b in range(1, NB):
@@ -105,11 +107,14 @@ def tile_mixtureofattentionheadssharedkv_t_kernel(tc, x, a, k, u, v_bytes, v_sca
 
         def v_widen():
             for e in range(E):
-                nc.tensor.matmul(ub[e][:].rearrange("p (h q c) -> p h q c", h=2, c=2), lhsT=sgn[:],
+                nc.tensor.matmul(ub[:, e, :].rearrange("p (h q c) -> p h q c", h=2, c=2), lhsT=sgn[:],
                                  rhs=ue[:, e, :].rearrange("p (q h c) -> p h q c", h=2, c=2), start=True, stop=True)
             for t in range(4):
                 nc.scalar.activation(out=vpl[:, t, :], in_=vb[:, t, :].bitcast(FP8), func=ACT.Copy, scale=vs[:, t:t + 1])
-            nc.gpsimd.tensor_scalar(out=vil[:], in0=vpl[:].rearrange("p t d -> p d t"), scalar1=1.0, scalar2=0.0, op0=ALU.mult, op1=ALU.add)
+
+        def v_interleave(h):
+            cols = slice(h * D // 2, (h + 1) * D // 2)
+            nc.scalar.copy(out=vil[:, cols, :], in_=vpl[:, :, cols].rearrange("p t d -> p d t"))
 
         def v_quant():
             nc.vector.quantize_mx(out=vc[:].bitcast(X4), scales=vq[:], in_=vil[:].rearrange("p d t -> p (d t)"))
@@ -122,45 +127,49 @@ def tile_mixtureofattentionheadssharedkv_t_kernel(tc, x, a, k, u, v_bytes, v_sca
             return st[name, i]
 
         def x_transpose(i):
-            words = xb[i // TB][:, i % TB, :].bitcast(F32)
-            for h in range(2):
-                nc.tensor.transpose(xz[:, h * P:(h + 1) * P], words[:, h::2], ident[:])
+            bank = x_bank.get(i // 2, xp)
+            for j in range(2):
+                words = xb[i // TB][:, i % TB + j, :].bitcast(F32)
+                for h in range(2):
+                    nc.tensor.transpose(bank[:, (2 * h + j) * P:(2 * h + j + 1) * P], words[:, h::2], ident[:])
 
         def x_copy(i):
-            nc.scalar.copy(out=buf("xts", i, [P, 2 * P], F32, 4, 64)[:], in_=xz[:, 0:2 * P])
+            nc.scalar.copy(out=buf("xts", i // 2, [P, 4 * P], F32, 5, 64)[:], in_=x_bank.get(i // 2, xp)[:])
 
         def q_mult(i, e):
-            qb = buf("qb", i, [P, E, P, 4], BF16, 2, 64)
+            qb = buf("qb", i // 2, [P, E, 2 * P, 4], BF16, 2, 64)
             nc.vector.tensor_tensor(
                 out=qb[:, e].rearrange("p r (h c) -> p r h c", c=2),
-                in0=xz[:, 0:2 * P].bitcast(BF16).rearrange("p (h r c) -> p r h c", h=2, c=2),
-                in1=aT[:, e, :].rearrange("p (h c) -> p h c", c=2).unsqueeze(1).to_broadcast([P, P, 2, 2]),
+                in0=x_bank.get(i // 2, xp)[:].bitcast(BF16).rearrange("p (h r c) -> p r h c", h=2, c=2),
+                in1=aT[:, e, :].rearrange("p (h c) -> p h c", c=2).unsqueeze(1).to_broadcast([P, 2 * P, 2, 2]),
                 op=ALU.mult)
 
         def q_quant(i):
-            nc.vector.quantize_mx(out=buf("qc", i, [P, E * P], U32, 4, 64)[:].bitcast(X4),
-                                  scales=buf("qs", i, [P, E * P], U8, 4, 64)[:],
-                                  in_=st["qb", i][:].rearrange("p e r t -> p (e r t)"))
+            nc.vector.quantize_mx(out=buf("qc", i // 2, [P, E * 2 * P], U32, 5, 64)[:].bitcast(X4),
+                                  scales=buf("qs", i // 2, [P, E * 2 * P], U8, 5, 64)[:],
+                                  in_=st["qb", i // 2][:].rearrange("p e r t -> p (e r t)"))
 
         def gates(i):
-            z = xz[:, 2 * P + (i % 4) * G:2 * P + (i % 4 + 1) * G]
-            xt = st["xts", i][:].bitcast(BF16).rearrange("p (h r c) -> p h c r", h=2, c=2)
-            nc.tensor.matmul(z, lhsT=sgn[:], rhs=brow[:], start=True, stop=False)
-            for t in range(4):
-                nc.tensor.matmul(z, lhsT=xt[:, t // 2, t % 2, :], rhs=w_sb[:, t, 0, :], start=False, stop=False)
-                nc.tensor.matmul(z, lhsT=xt[:, t // 2, t % 2, :], rhs=wn[:, t, :], start=False, stop=(t == 3))
+            xt = st["xts", i // 2][:].bitcast(BF16).rearrange("p (h r c) -> p h c r", h=2, c=2)
+            for j in range(2):
+                z = zs[:, (i + j) % 8, :]
+                rows = slice(j * P, (j + 1) * P)
+                nc.tensor.matmul(z, lhsT=sgn[:], rhs=brow[:], start=True, stop=False)
+                for t in range(4):
+                    nc.tensor.matmul(z, lhsT=xt[:, t // 2, t % 2, rows], rhs=w_sb[:, t, 0, :], start=False, stop=False)
+                    nc.tensor.matmul(z, lhsT=xt[:, t // 2, t % 2, rows], rhs=wn[:, t, :], start=False, stop=(t == 3))
 
         def gate_act(i):
-            if i % 2 == 1:
-                z = xz[:, 2 * P + (i % 4 - 1) * G:2 * P + (i % 4 + 1) * G]
-                th = buf("th", i // 2, [P, 2 * G], F32, 3)
-                nc.scalar.activation(out=th[:], in_=z, func=ACT.Tanh, scale=0.5)
-                nc.scalar.activation(out=buf("g", i // 2, [P, 2, G], F32, 4)[:].rearrange("p i j -> p (i j)"),
+            if i % 4 == 2:
+                f = i - 2
+                th = buf("th", i // 4, [P, 4 * G], F32, 2)
+                nc.scalar.activation(out=th[:], in_=zs[:, f % 8:f % 8 + 4, :].rearrange("p i j -> p (i j)"), func=ACT.Tanh, scale=0.5)
+                nc.scalar.activation(out=buf("g", i // 4, [P, 4, G], F32, 3)[:].rearrange("p i j -> p (i j)"),
                                      in_=th[:], func=ACT.Copy, scale=0.5, bias=0.5)
 
         def score(i, e):
-            cols = slice(e * P, (e + 1) * P)
-            nc.tensor.matmul_mx(out=sc[e][:], lhsT=st["qc", i][:, cols].bitcast(X4), lhsT_scale=st["qs", i][:, cols],
+            cols = slice((2 * e + i % 2) * P, (2 * e + i % 2 + 1) * P)
+            nc.tensor.matmul_mx(out=sc[e][:], lhsT=st["qc", i // 2][:, cols].bitcast(X4), lhsT_scale=st["qs", i // 2][:, cols],
                                 rhs=kc[:].bitcast(X4), rhs_scale=kq[:], start=True, stop=True)
 
         def row_max(i, e):
@@ -178,7 +187,7 @@ def tile_mixtureofattentionheadssharedkv_t_kernel(tc, x, a, k, u, v_bytes, v_sca
 
         def p_mult(i, e):
             nc.vector.scalar_tensor_tensor(out=buf("pu%d" % e, i, [P, M], BF16, 2)[:], in0=st["ee%d" % e, i][:],
-                                           scalar=st["ri", i][:, e:e + 1], in1=ub[e][:], op0=ALU.mult, op1=ALU.mult)
+                                           scalar=st["ri", i][:, e:e + 1], in1=ub[:, e, :], op0=ALU.mult, op1=ALU.mult)
 
         def p_transpose(i, e):
             words = st["pu%d" % e, i][:].bitcast(F32)
@@ -220,7 +229,7 @@ def tile_mixtureofattentionheadssharedkv_t_kernel(tc, x, a, k, u, v_bytes, v_sca
             eng.tensor_tensor(
                 out=buf("t", i, [P, D], F32, 3)[:].rearrange("p (j c) -> p j c", c=8),
                 in0=(od if tail else st["ds", i])[:].rearrange("p (j c) -> p j c", c=8),
-                in1=st["g", i // 2][:, i % 2, :].unsqueeze(2).to_broadcast([P, G, 8]), op=ALU.mult)
+                in1=st["g", i // 4][:, i % 4, :].unsqueeze(2).to_broadcast([P, G, 8]), op=ALU.mult)
 
         def gate_sub(i):
             r = buf("r", i, [P, D], F32, 4)
@@ -236,11 +245,12 @@ def tile_mixtureofattentionheadssharedkv_t_kernel(tc, x, a, k, u, v_bytes, v_sca
             "pm0": (p_mult, 0), "pm1": (p_mult, 1), "pt0": (p_transpose, 0), "pt1": (p_transpose, 1), "pc": (p_copy,), "pq": (p_quant,),
             "oD": (out_diff,), "oO": (out_one,), "cD": (diff_copy,), "cO": (one_copy,), "gm": (gate_mult,), "gs": (gate_sub,),
         }
-        order = [("pt1", 5), ("ex0", 4), ("mx1", 3), ("pm0", 5), ("xc", 1), ("oO", 7), ("sc0", 3), ("rc", 4), ("qq", 2), ("ga", 6), ("pq", 6), ("nm1", 3), ("mx0", 3), ("cD", 7), ("ex1", 3), ("gm", 7), ("cO", 7), ("gt", 4), ("pt0", 5), ("gs", 7), ("xT", 0), ("sc1", 2), ("pm1", 4), ("oD", 6), ("nm0", 3), ("pc", 5), ("qm1", 0), ("qm0", 0)]
-        prologue = {0: k_transpose, 1: k_quant, 2: v_widen, 4: v_quant}
+        order = [("qq", 2), ("pt1", 5), ("xT", 0), ("mx0", 3), ("gm", 7), ("qm0", 1), ("pt0", 5), ("sc1", 3), ("rc", 4), ("qm1", 0), ("ga", 4), ("mx1", 3), ("cO", 7), ("nm0", 3), ("pc", 5), ("ex0", 3), ("gs", 7), ("nm1", 3), ("oD", 6), ("cD", 6), ("oO", 6), ("pm1", 4), ("xc", 1), ("pm0", 4), ("gt", 3), ("ex1", 3), ("pq", 5), ("sc0", 2)]
+        paired = ("xT", "xc", "qm0", "qm1", "qq", "gt", "ga")
+        prologue = {0: (k_transpose,), 1: (k_quant,), 2: (v_widen,), 3: (v_interleave, 0), 4: (v_interleave, 1), 5: (v_quant,)}
         for n in range(NT + max(lag for name, lag in order)):
             for name, lag in order:
-                if 0 <= n - lag < NT:
+                if 0 <= n - lag < NT and ((n - lag) % 2 == 0 or name not in paired):
                     stages[name][0](n - lag, *stages[name][1:])
             if n in prologue:
-                prologue[n]()
+                prologue[n][0](*prologue[n][1:])

@@ -39,7 +39,7 @@ def tile_mixtureofattentionheadssharedkv_t_kernel(tc, x, a, k, u, v_bytes, v_sca
         o1 = psum.tile([P, D], F32, name="o1")
         xp = psum.tile([P, 2 * 2 * P], F32, name="xp")
         zs = psum.tile([P, 8, G], F32, name="zs")
-        x_bank = {1: od, 2: o1}
+        x_bank = {1: od}
 
         k_sb = keep.tile([P, 4, D], BF16, name="k_sb")
         aT = keep.tile([P, E, 4], BF16, name="aT")
@@ -65,6 +65,7 @@ def tile_mixtureofattentionheadssharedkv_t_kernel(tc, x, a, k, u, v_bytes, v_sca
         xb = [keep.tile([P, TB, D], BF16, name="xb%d" % b) for b in range(NB)]
 
         k_rows = k.rearrange("(p j) d -> p j d", j=4)
+        nc.sync.dma_start(out=aT[:], in_=a.rearrange("e (p t) -> p e t", t=4))
         nc.sync.dma_start(out=xb[0][:, 0:2, :], in_=x_blocks[0][:, 0:2, :])
         nc.sync.dma_start(out=k_sb[:, 0:2, :], in_=k_rows[:, 0:2, :])
         nc.sync.dma_start(out=k_sb[:, 2:4, :], in_=k_rows[:, 2:4, :])
@@ -80,13 +81,12 @@ def tile_mixtureofattentionheadssharedkv_t_kernel(tc, x, a, k, u, v_bytes, v_sca
         nc.gpsimd.memset(brow[:], 0.0)
         nc.gpsimd.memset(sgn[:], -1.0)
         nc.gpsimd.memset(sgn[0:32, :], 1.0)
-        nc.scalar.activation(out=warm[:], in_=warm[:], func=ACT.Exp)
-        nc.scalar.dma_start(out=aT[:], in_=a.rearrange("e (p t) -> p e t", t=4))
         nc.scalar.dma_start(out=ue[0:1, 0, :], in_=u[0:1, :])
         nc.scalar.dma_start(out=ue[32:33, 1, :], in_=u[1:2, :])
         nc.scalar.dma_start(out=brow[0:1, :], in_=bg[0:1, :])
         nc.scalar.dma_start(out=brow[32:33, :], in_=bg[1:2, :])
         nc.scalar.dma_start(out=vs[:], in_=v_scale.rearrange("(p t) o -> p (t o)", t=4))
+        nc.scalar.activation(out=warm[:], in_=warm[:], func=ACT.Exp)
 
         nc.gpsimd.tensor_scalar(out=wn[:], in0=w_sb[:, :, 1, :], scalar1=-1.0, scalar2=0.0, op0=ALU.mult, op1=ALU.add)
 
@@ -137,7 +137,7 @@ def tile_mixtureofattentionheadssharedkv_t_kernel(tc, x, a, k, u, v_bytes, v_sca
             nc.scalar.copy(out=buf("xts", i // 2, [P, 4 * P], F32, 5, 64)[:], in_=x_bank.get(i // 2, xp)[:])
 
         def q_mult(i, e):
-            qb = buf("qb", i // 2, [P, E, 2 * P, 4], BF16, 2, 64)
+            qb = buf("qb", i // 2, [P, E, 2 * P, 4], BF16, 3, 64)
             nc.vector.tensor_tensor(
                 out=qb[:, e].rearrange("p r (h c) -> p r h c", c=2),
                 in0=x_bank.get(i // 2, xp)[:].bitcast(BF16).rearrange("p (h r c) -> p r h c", h=2, c=2),
@@ -151,21 +151,23 @@ def tile_mixtureofattentionheadssharedkv_t_kernel(tc, x, a, k, u, v_bytes, v_sca
 
         def gates(i):
             xt = st["xts", i // 2][:].bitcast(BF16).rearrange("p (h r c) -> p h c r", h=2, c=2)
-            for j in range(2):
-                z = zs[:, (i + j) % 8, :]
-                rows = slice(j * P, (j + 1) * P)
-                nc.tensor.matmul(z, lhsT=sgn[:], rhs=brow[:], start=True, stop=False)
-                for t in range(4):
-                    nc.tensor.matmul(z, lhsT=xt[:, t // 2, t % 2, rows], rhs=w_sb[:, t, 0, :], start=False, stop=False)
-                    nc.tensor.matmul(z, lhsT=xt[:, t // 2, t % 2, rows], rhs=wn[:, t, :], start=False, stop=(t == 3))
+            rows = slice(i % 2 * P, (i % 2 + 1) * P)
+            if i % 4 == 0:
+                nc.tensor.matmul(zs[:, i % 8:i % 8 + 4, :], lhsT=sgn[:], rhs=brow[:].unsqueeze(1).to_broadcast([P, 4, G]),
+                                 start=True, stop=False)
+            for t in range(4):
+                x_cols = xt[:, t // 2, t % 2, rows]
+                nc.tensor.matmul(zs[:, i % 8, :], lhsT=x_cols, rhs=w_sb[:, t, 0, :], start=False, stop=False)
+                nc.tensor.matmul(zs[:, i % 8, :], lhsT=x_cols, rhs=wn[:, t, :], start=False, stop=(i % 4 == 3 and t == 3))
 
         def gate_act(i):
-            if i % 4 == 2:
-                f = i - 2
-                th = buf("th", i // 4, [P, 4 * G], F32, 2)
-                nc.scalar.activation(out=th[:], in_=zs[:, f % 8:f % 8 + 4, :].rearrange("p i j -> p (i j)"), func=ACT.Tanh, scale=0.5)
-                nc.scalar.activation(out=buf("g", i // 4, [P, 4, G], F32, 3)[:].rearrange("p i j -> p (i j)"),
-                                     in_=th[:], func=ACT.Copy, scale=0.5, bias=0.5)
+            f = (i - 3) % 8
+            th = buf("th", i // 4, [P, 4 * G], F32, 2)
+            nc.scalar.activation(out=th[:], in_=zs[:, f:f + 4, :].rearrange("p i j -> p (i j)"), func=ACT.Tanh, scale=0.5)
+
+        def gate_affine(i):
+            nc.gpsimd.tensor_scalar(out=buf("g", i // 4, [P, 4, G], F32, 3)[:].rearrange("p i j -> p (i j)"),
+                                    in0=st["th", i // 4][:], scalar1=0.5, scalar2=0.5, op0=ALU.mult, op1=ALU.add)
 
         def score(i, e):
             cols = slice((2 * e + i % 2) * P, (2 * e + i % 2 + 1) * P)
@@ -179,14 +181,14 @@ def tile_mixtureofattentionheadssharedkv_t_kernel(tc, x, a, k, u, v_bytes, v_sca
             nc.scalar.activation(out=buf("nm%d" % e, i, [P, 1], F32, 4)[:], in_=st["mx%d" % e, i][:], func=ACT.Copy, scale=-SCALE)
 
         def exp(i, e):
-            nc.scalar.activation(out=buf("ee%d" % e, i, [P, M], F32, 2)[:], in_=sc[e][:], func=ACT.Exp, scale=SCALE,
+            nc.scalar.activation(out=buf("ee%d" % e, i, [P, M], F32, 4)[:], in_=sc[e][:], func=ACT.Exp, scale=SCALE,
                                  bias=st["nm%d" % e, i][:], accum_out=buf("rs", i, [P, E], F32, 4)[:, e:e + 1])
 
         def recip(i):
             nc.vector.reciprocal(buf("ri", i, [P, E], F32, 4)[:], st["rs", i][:])
 
         def p_mult(i, e):
-            nc.vector.scalar_tensor_tensor(out=buf("pu%d" % e, i, [P, M], BF16, 2)[:], in0=st["ee%d" % e, i][:],
+            nc.vector.scalar_tensor_tensor(out=buf("pu%d" % e, i, [P, M], BF16, 3)[:], in0=st["ee%d" % e, i][:],
                                            scalar=st["ri", i][:, e:e + 1], in1=ub[:, e, :], op0=ALU.mult, op1=ALU.mult)
 
         def p_transpose(i, e):
@@ -196,12 +198,12 @@ def tile_mixtureofattentionheadssharedkv_t_kernel(tc, x, a, k, u, v_bytes, v_sca
                 nc.tensor.transpose(pt[:, col:col + P], words[:, h * P:(h + 1) * P], ident[:])
 
         def p_copy(i):
-            nc.scalar.copy(out=buf("pT", i, [P, E * P * 4], BF16, 2, 64)[:].bitcast(F32).rearrange("p (e r h) -> p e r h", e=E, h=2),
+            nc.scalar.copy(out=buf("pT", i, [P, E * P * 4], BF16, 3, 64)[:].bitcast(F32).rearrange("p (e r h) -> p e r h", e=E, h=2),
                            in_=pt[:].rearrange("p (e h r) -> p e r h", e=E, h=2))
 
         def p_quant(i):
-            nc.vector.quantize_mx(out=buf("pc", i, [P, E * P], U32, 2, 64)[:].bitcast(X4),
-                                  scales=buf("ps", i, [P, E * P], U8, 2, 64)[:], in_=st["pT", i][:])
+            nc.vector.quantize_mx(out=buf("pc", i, [P, E * P], U32, 3, 64)[:].bitcast(X4),
+                                  scales=buf("ps", i, [P, E * P], U8, 3, 64)[:], in_=st["pT", i][:])
 
         def out_mm(i, dst, e, first, last):
             cols = slice(e * P, (e + 1) * P)
@@ -217,11 +219,11 @@ def tile_mixtureofattentionheadssharedkv_t_kernel(tc, x, a, k, u, v_bytes, v_sca
 
         def diff_copy(i):
             if i < NT - TV:
-                nc.scalar.copy(out=buf("ds", i, [P, D], F32, 2)[:], in_=od[:])
+                nc.scalar.copy(out=buf("ds", i, [P, D], F32, 3)[:], in_=od[:])
 
         def one_copy(i):
             if i < NT - TV:
-                nc.scalar.copy(out=buf("oc", i, [P, D], F32, 2)[:], in_=o1[:])
+                nc.scalar.copy(out=buf("oc", i, [P, D], F32, 3)[:], in_=o1[:])
 
         def gate_mult(i):
             tail = i >= NT - TV
@@ -240,17 +242,17 @@ def tile_mixtureofattentionheadssharedkv_t_kernel(tc, x, a, k, u, v_bytes, v_sca
 
         stages = {
             "xT": (x_transpose,), "xc": (x_copy,), "qm0": (q_mult, 0), "qm1": (q_mult, 1), "qq": (q_quant,),
-            "gt": (gates,), "ga": (gate_act,), "sc0": (score, 0), "sc1": (score, 1), "mx0": (row_max, 0), "mx1": (row_max, 1),
+            "gt": (gates,), "ga": (gate_act,), "gf": (gate_affine,), "sc0": (score, 0), "sc1": (score, 1), "mx0": (row_max, 0), "mx1": (row_max, 1),
             "nm0": (neg_max, 0), "nm1": (neg_max, 1), "ex0": (exp, 0), "ex1": (exp, 1), "rc": (recip,),
             "pm0": (p_mult, 0), "pm1": (p_mult, 1), "pt0": (p_transpose, 0), "pt1": (p_transpose, 1), "pc": (p_copy,), "pq": (p_quant,),
             "oD": (out_diff,), "oO": (out_one,), "cD": (diff_copy,), "cO": (one_copy,), "gm": (gate_mult,), "gs": (gate_sub,),
         }
-        order = [("qq", 2), ("pt1", 5), ("xT", 0), ("mx0", 3), ("gm", 7), ("qm0", 1), ("pt0", 5), ("sc1", 3), ("rc", 4), ("qm1", 0), ("ga", 4), ("mx1", 3), ("cO", 7), ("nm0", 3), ("pc", 5), ("ex0", 3), ("gs", 7), ("nm1", 3), ("oD", 6), ("cD", 6), ("oO", 6), ("pm1", 4), ("xc", 1), ("pm0", 4), ("gt", 3), ("ex1", 3), ("pq", 5), ("sc0", 2)]
-        paired = ("xT", "xc", "qm0", "qm1", "qq", "gt", "ga")
+        order = [("mx0", 3), ("cO", 8), ("pt0", 5), ("sc1", 3), ("pq", 6), ("qq", 2), ("xT", 0), ("gf", 3), ("nm0", 3), ("cD", 7), ("rc", 4), ("qm0", 1), ("ex0", 3), ("gs", 8), ("xc", 0), ("gm", 7), ("mx1", 3), ("gt", 2), ("ga", 2), ("pm1", 4), ("nm1", 3), ("oO", 7), ("sc0", 2), ("pm0", 4), ("qm1", 0), ("oD", 6), ("pc", 5), ("pt1", 4), ("ex1", 3)]
+        period = {"xT": (2, 0), "xc": (2, 0), "qm0": (2, 0), "qm1": (2, 0), "qq": (2, 0), "ga": (4, 3), "gf": (4, 3)}
         prologue = {0: (k_transpose,), 1: (k_quant,), 2: (v_widen,), 3: (v_interleave, 0), 4: (v_interleave, 1), 5: (v_quant,)}
         for n in range(NT + max(lag for name, lag in order)):
             for name, lag in order:
-                if 0 <= n - lag < NT and ((n - lag) % 2 == 0 or name not in paired):
+                if 0 <= n - lag < NT and (n - lag) % period.get(name, (1, 0))[0] == period.get(name, (1, 0))[1]:
                     stages[name][0](n - lag, *stages[name][1:])
             if n in prologue:
                 prologue[n][0](*prologue[n][1:])

@@ -65,29 +65,27 @@ def tile_mixtureofattentionheadssharedkv_t_kernel(tc, x, a, k, u, v_bytes, v_sca
         xb = [keep.tile([P, TB, D], BF16, name="xb%d" % b) for b in range(NB)]
 
         k_rows = k.rearrange("(p j) d -> p j d", j=4)
-        nc.sync.dma_start(out=aT[:], in_=a.rearrange("e (p t) -> p e t", t=4))
+        nc.vector.memset(warm[:], 0.0)
+        nc.scalar.activation(out=warm[:], in_=warm[:], func=ACT.Exp)
         nc.sync.dma_start(out=xb[0][:, 0:2, :], in_=x_blocks[0][:, 0:2, :])
         nc.sync.dma_start(out=k_sb[:, 0:2, :], in_=k_rows[:, 0:2, :])
         nc.sync.dma_start(out=k_sb[:, 2:4, :], in_=k_rows[:, 2:4, :])
+        nc.scalar.dma_start(out=aT[:], in_=a.rearrange("e (p t) -> p e t", t=4))
         nc.sync.dma_start(out=xb[0][:, 2:4, :], in_=x_blocks[0][:, 2:4, :])
+        make_identity(nc, ident[:])
+        nc.vector.memset(ue[:], 0.0)
+        nc.vector.memset(brow[:], 0.0)
+        nc.gpsimd.memset(sgn[:], -1.0)
+        nc.gpsimd.memset(sgn[0:32, :], 1.0)
+        nc.sync.dma_start(out=ue[0:1, 0, :], in_=u[0:1, :])
+        nc.sync.dma_start(out=ue[32:33, 1, :], in_=u[1:2, :])
+        nc.sync.dma_start(out=vs[:], in_=v_scale.rearrange("(p t) o -> p (t o)", t=4))
         nc.sync.dma_start(out=vb[:], in_=v_bytes.rearrange("(p t) d -> p t d", t=4))
+        nc.sync.dma_start(out=brow[0:1, :], in_=bg[0:1, :])
+        nc.sync.dma_start(out=brow[32:33, :], in_=bg[1:2, :])
         nc.sync.dma_start(out=w_sb[:], in_=wg.rearrange("(p t) e j -> p t e j", t=4))
         for b in range(1, NB):
             nc.sync.dma_start(out=xb[b][:], in_=x_blocks[b])
-
-        nc.vector.memset(warm[:], 0.0)
-        nc.vector.memset(ue[:], 0.0)
-        make_identity(nc, ident[:])
-        nc.gpsimd.memset(brow[:], 0.0)
-        nc.gpsimd.memset(sgn[:], -1.0)
-        nc.gpsimd.memset(sgn[0:32, :], 1.0)
-        nc.scalar.dma_start(out=ue[0:1, 0, :], in_=u[0:1, :])
-        nc.scalar.dma_start(out=ue[32:33, 1, :], in_=u[1:2, :])
-        nc.scalar.dma_start(out=brow[0:1, :], in_=bg[0:1, :])
-        nc.scalar.dma_start(out=brow[32:33, :], in_=bg[1:2, :])
-        nc.scalar.dma_start(out=vs[:], in_=v_scale.rearrange("(p t) o -> p (t o)", t=4))
-        nc.scalar.activation(out=warm[:], in_=warm[:], func=ACT.Exp)
-
         nc.gpsimd.tensor_scalar(out=wn[:], in0=w_sb[:, :, 1, :], scalar1=-1.0, scalar2=0.0, op0=ALU.mult, op1=ALU.add)
 
         def k_transpose():

from contextlib import ExitStack

import concourse.mybir as mybir
from concourse.masks import make_identity

S, D, M, E, G = 4096, 512, 512, 2, 64
FLOPS = 2 * S * (2 * E * D * M + D * E * G)

F32 = mybir.dt.float32
BF16 = mybir.dt.bfloat16
U32 = mybir.dt.uint32
U8 = mybir.dt.uint8
X4 = mybir.dt.float8_e4m3fn_x4
FP8 = mybir.dt.float8_e4m3fn
ALU = mybir.AluOpType
ACT = mybir.ActivationFunctionType
AX = mybir.AxisListType

P = 128
NT = S // P
TB = 4
NB = NT // TB
TV = 4
SCALE = 1.0 / float(D) ** 0.5


def tile_mixtureofattentionheadssharedkv_t_kernel(tc, x, a, k, u, v_bytes, v_scale, wg, bg, out):
    nc = tc.nc
    with ExitStack() as ctx:
        keep = ctx.enter_context(tc.tile_pool(name="keep", bufs=1))
        work = ctx.enter_context(tc.tile_pool(name="work", bufs=4))
        psum = ctx.enter_context(tc.psum_pool(name="psum", bufs=1))
        ctx.enter_context(tc.manual_schedule())

        sc = [psum.tile([P, M], F32, name="sc0"), psum.tile([P, M], F32, name="sc1")]
        ub = psum.tile([P, E, M], BF16, name="ub")
        pt = psum.tile([P, M], F32, name="pt")
        od = psum.tile([P, D], F32, name="od")
        o1 = psum.tile([P, D], F32, name="o1")
        xp = psum.tile([P, 2 * 2 * P], F32, name="xp")
        zs = psum.tile([P, 8, G], F32, name="zs")
        x_bank = {1: od}

        k_sb = keep.tile([P, 4, D], BF16, name="k_sb")
        aT = keep.tile([P, E, 4], BF16, name="aT")
        w_sb = keep.tile([P, 4, E, G], BF16, name="w_sb")
        wn = keep.tile([P, 4, G], BF16, name="wn")
        ue = keep.tile([P, E, M], BF16, name="ue")
        sgn = keep.tile([P, P], BF16, name="sgn")
        brow = keep.tile([P, G], BF16, name="brow")
        ident = keep.tile([P, P], F32, name="ident")
        vb = keep.tile([P, 4, D], U8, name="vb")
        vs = keep.tile([P, 4], F32, name="vs")
        vpl = keep.tile([P, 4, D], BF16, name="vpl", align_bytes=64)
        vil = keep.tile([P, D, 4], BF16, name="vil", align_bytes=64)
        vc = keep.tile([P, D], U32, name="vc", align_bytes=64)
        vq = keep.tile([P, D], U8, name="vq", align_bytes=64)
        kil = keep.tile([P, M * 4], BF16, name="kil", align_bytes=64)
        kc = keep.tile([P, M], U32, name="kc", align_bytes=64)
        kq = keep.tile([P, M], U8, name="kq", align_bytes=64)
        warm = keep.tile([P, 1], F32, name="warm")

        x_blocks = x.rearrange("(b p j) d -> b p j d", p=P, j=TB)
        out_blocks = out.rearrange("(b p j) d -> b p j d", p=P, j=TB)
        xb = [keep.tile([P, TB, D], BF16, name="xb%d" % b) for b in range(NB)]

        k_rows = k.rearrange("(p j) d -> p j d", j=4)
        nc.vector.memset(warm[:], 0.0)
        nc.scalar.activation(out=warm[:], in_=warm[:], func=ACT.Exp)
        nc.sync.dma_start(out=xb[0][:, 0:2, :], in_=x_blocks[0][:, 0:2, :])
        nc.sync.dma_start(out=k_sb[:, 0:2, :], in_=k_rows[:, 0:2, :])
        nc.sync.dma_start(out=k_sb[:, 2:4, :], in_=k_rows[:, 2:4, :])
        nc.scalar.dma_start(out=aT[:], in_=a.rearrange("e (p t) -> p e t", t=4))
        nc.sync.dma_start(out=xb[0][:, 2:4, :], in_=x_blocks[0][:, 2:4, :])
        make_identity(nc, ident[:])
        nc.vector.memset(ue[:], 0.0)
        nc.vector.memset(brow[:], 0.0)
        nc.gpsimd.memset(sgn[:], -1.0)
        nc.gpsimd.memset(sgn[0:32, :], 1.0)
        nc.sync.dma_start(out=ue[0:1, 0, :], in_=u[0:1, :])
        nc.sync.dma_start(out=ue[32:33, 1, :], in_=u[1:2, :])
        nc.sync.dma_start(out=vs[:], in_=v_scale.rearrange("(p t) o -> p (t o)", t=4))
        nc.sync.dma_start(out=vb[:], in_=v_bytes.rearrange("(p t) d -> p t d", t=4))
        nc.sync.dma_start(out=brow[0:1, :], in_=bg[0:1, :])
        nc.sync.dma_start(out=brow[32:33, :], in_=bg[1:2, :])
        nc.sync.dma_start(out=w_sb[:], in_=wg.rearrange("(p t) e j -> p t e j", t=4))
        for b in range(1, NB):
            nc.sync.dma_start(out=xb[b][:], in_=x_blocks[b])
        nc.gpsimd.tensor_scalar(out=wn[:], in0=w_sb[:, :, 1, :], scalar1=-1.0, scalar2=0.0, op0=ALU.mult, op1=ALU.add)

        def k_transpose():
            for j in range(4):
                words = k_sb[:, j, :].bitcast(F32)
                for h in range(2):
                    col = ((j % 2) * 2 + h) * P
                    nc.tensor.transpose(sc[j // 2][:, col:col + P], words[:, h::2], ident[:])
            kw = kil[:].bitcast(F32).rearrange("p (u r c h) -> p u r c h", u=2, c=2, h=2)
            nc.vector.tensor_copy(out=kw[:, 0], in_=sc[0][:].rearrange("p (c h r) -> p r c h", c=2, h=2))
            nc.scalar.copy(out=kw[:, 1], in_=sc[1][:].rearrange("p (c h r) -> p r c h", c=2, h=2))

        def k_quant():
            for h in range(2):
                nc.vector.quantize_mx(out=kc[:, h * 256:(h + 1) * 256].bitcast(X4), scales=kq[:, h * 256:(h + 1) * 256],
                                      in_=kil[:, h * 1024:(h + 1) * 1024])

        def v_widen():
            for e in range(E):
                nc.tensor.matmul(ub[:, e, :].rearrange("p (h q c) -> p h q c", h=2, c=2), lhsT=sgn[:],
                                 rhs=ue[:, e, :].rearrange("p (q h c) -> p h q c", h=2, c=2), start=True, stop=True)
            for t in range(4):
                nc.scalar.activation(out=vpl[:, t, :], in_=vb[:, t, :].bitcast(FP8), func=ACT.Copy, scale=vs[:, t:t + 1])

        def v_interleave(h):
            cols = slice(h * D // 2, (h + 1) * D // 2)
            nc.scalar.copy(out=vil[:, cols, :], in_=vpl[:, :, cols].rearrange("p t d -> p d t"))

        def v_quant():
            nc.vector.quantize_mx(out=vc[:].bitcast(X4), scales=vq[:], in_=vil[:].rearrange("p d t -> p (d t)"))

        st = {}

        def buf(name, i, shape, dtype, bufs, align=32):
            if (name, i) not in st:
                st[name, i] = work.tile(shape, dtype, name=name, bufs=bufs, align_bytes=align)
            return st[name, i]

        def x_transpose(i):
            bank = x_bank.get(i // 2, xp)
            for j in range(2):
                words = xb[i // TB][:, i % TB + j, :].bitcast(F32)
                for h in range(2):
                    nc.tensor.transpose(bank[:, (2 * h + j) * P:(2 * h + j + 1) * P], words[:, h::2], ident[:])

        def x_copy(i):
            nc.scalar.copy(out=buf("xts", i // 2, [P, 4 * P], F32, 5, 64)[:], in_=x_bank.get(i // 2, xp)[:])

        def q_mult(i, e):
            qb = buf("qb", i // 2, [P, E, 2 * P, 4], BF16, 3, 64)
            nc.vector.tensor_tensor(
                out=qb[:, e].rearrange("p r (h c) -> p r h c", c=2),
                in0=x_bank.get(i // 2, xp)[:].bitcast(BF16).rearrange("p (h r c) -> p r h c", h=2, c=2),
                in1=aT[:, e, :].rearrange("p (h c) -> p h c", c=2).unsqueeze(1).to_broadcast([P, 2 * P, 2, 2]),
                op=ALU.mult)

        def q_quant(i):
            nc.vector.quantize_mx(out=buf("qc", i // 2, [P, E * 2 * P], U32, 5, 64)[:].bitcast(X4),
                                  scales=buf("qs", i // 2, [P, E * 2 * P], U8, 5, 64)[:],
                                  in_=st["qb", i // 2][:].rearrange("p e r t -> p (e r t)"))

        def gates(i):
            xt = st["xts", i // 2][:].bitcast(BF16).rearrange("p (h r c) -> p h c r", h=2, c=2)
            rows = slice(i % 2 * P, (i % 2 + 1) * P)
            if i % 4 == 0:
                nc.tensor.matmul(zs[:, i % 8:i % 8 + 4, :], lhsT=sgn[:], rhs=brow[:].unsqueeze(1).to_broadcast([P, 4, G]),
                                 start=True, stop=False)
            for t in range(4):
                x_cols = xt[:, t // 2, t % 2, rows]
                nc.tensor.matmul(zs[:, i % 8, :], lhsT=x_cols, rhs=w_sb[:, t, 0, :], start=False, stop=False)
                nc.tensor.matmul(zs[:, i % 8, :], lhsT=x_cols, rhs=wn[:, t, :], start=False, stop=(i % 4 == 3 and t == 3))

        def gate_act(i):
            f = (i - 3) % 8
            th = buf("th", i // 4, [P, 4 * G], F32, 2)
            nc.scalar.activation(out=th[:], in_=zs[:, f:f + 4, :].rearrange("p i j -> p (i j)"), func=ACT.Tanh, scale=0.5)

        def gate_affine(i):
            nc.gpsimd.tensor_scalar(out=buf("g", i // 4, [P, 4, G], F32, 3)[:].rearrange("p i j -> p (i j)"),
                                    in0=st["th", i // 4][:], scalar1=0.5, scalar2=0.5, op0=ALU.mult, op1=ALU.add)

        def score(i, e):
            cols = slice((2 * e + i % 2) * P, (2 * e + i % 2 + 1) * P)
            nc.tensor.matmul_mx(out=sc[e][:], lhsT=st["qc", i // 2][:, cols].bitcast(X4), lhsT_scale=st["qs", i // 2][:, cols],
                                rhs=kc[:].bitcast(X4), rhs_scale=kq[:], start=True, stop=True)

        def row_max(i, e):
            nc.vector.tensor_reduce(out=buf("mx%d" % e, i, [P, 1], F32, 4)[:], in_=sc[e][:], axis=AX.X, op=ALU.max)

        def neg_max(i, e):
            nc.scalar.activation(out=buf("nm%d" % e, i, [P, 1], F32, 4)[:], in_=st["mx%d" % e, i][:], func=ACT.Copy, scale=-SCALE)

        def exp(i, e):
            nc.scalar.activation(out=buf("ee%d" % e, i, [P, M], F32, 4)[:], in_=sc[e][:], func=ACT.Exp, scale=SCALE,
                                 bias=st["nm%d" % e, i][:], accum_out=buf("rs", i, [P, E], F32, 4)[:, e:e + 1])

        def recip(i):
            nc.vector.reciprocal(buf("ri", i, [P, E], F32, 4)[:], st["rs", i][:])

        def p_mult(i, e):
            nc.vector.scalar_tensor_tensor(out=buf("pu%d" % e, i, [P, M], BF16, 3)[:], in0=st["ee%d" % e, i][:],
                                           scalar=st["ri", i][:, e:e + 1], in1=ub[:, e, :], op0=ALU.mult, op1=ALU.mult)

        def p_transpose(i, e):
            words = st["pu%d" % e, i][:].bitcast(F32)
            for h in range(2):
                col = (e * 2 + h) * P
                nc.tensor.transpose(pt[:, col:col + P], words[:, h * P:(h + 1) * P], ident[:])

        def p_copy(i):
            nc.scalar.copy(out=buf("pT", i, [P, E * P * 4], BF16, 3, 64)[:].bitcast(F32).rearrange("p (e r h) -> p e r h", e=E, h=2),
                           in_=pt[:].rearrange("p (e h r) -> p e r h", e=E, h=2))

        def p_quant(i):
            nc.vector.quantize_mx(out=buf("pc", i, [P, E * P], U32, 3, 64)[:].bitcast(X4),
                                  scales=buf("ps", i, [P, E * P], U8, 3, 64)[:], in_=st["pT", i][:])

        def out_mm(i, dst, e, first, last):
            cols = slice(e * P, (e + 1) * P)
            nc.tensor.matmul_mx(out=dst[:], lhsT=st["pc", i][:, cols].bitcast(X4), lhsT_scale=st["ps", i][:, cols],
                                rhs=vc[:].bitcast(X4), rhs_scale=vq[:], start=first, stop=last)

        def out_diff(i):
            out_mm(i, od, 0, True, False)
            out_mm(i, od, 1, False, True)

        def out_one(i):
            out_mm(i, o1, 1, True, True)

        def diff_copy(i):
            if i < NT - TV:
                nc.scalar.copy(out=buf("ds", i, [P, D], F32, 3)[:], in_=od[:])

        def one_copy(i):
            if i < NT - TV:
                nc.scalar.copy(out=buf("oc", i, [P, D], F32, 3)[:], in_=o1[:])

        def gate_mult(i):
            tail = i >= NT - TV
            eng = nc.vector if tail else nc.gpsimd
            eng.tensor_tensor(
                out=buf("t", i, [P, D], F32, 3)[:].rearrange("p (j c) -> p j c", c=8),
                in0=(od if tail else st["ds", i])[:].rearrange("p (j c) -> p j c", c=8),
                in1=st["g", i // 4][:, i % 4, :].unsqueeze(2).to_broadcast([P, G, 8]), op=ALU.mult)

        def gate_sub(i):
            r = buf("r", i, [P, D], F32, 4)
            tail = i >= NT - TV
            eng = nc.vector if tail else nc.gpsimd
            eng.tensor_tensor(out=r[:], in0=st["t", i][:], in1=(o1 if tail else st["oc", i])[:], op=ALU.subtract)
            nc.sync.dma_start(out=out_blocks[i // TB][:, i % TB, :], in_=r[:])

        stages = {
            "xT": (x_transpose,), "xc": (x_copy,), "qm0": (q_mult, 0), "qm1": (q_mult, 1), "qq": (q_quant,),
            "gt": (gates,), "ga": (gate_act,), "gf": (gate_affine,), "sc0": (score, 0), "sc1": (score, 1), "mx0": (row_max, 0), "mx1": (row_max, 1),
            "nm0": (neg_max, 0), "nm1": (neg_max, 1), "ex0": (exp, 0), "ex1": (exp, 1), "rc": (recip,),
            "pm0": (p_mult, 0), "pm1": (p_mult, 1), "pt0": (p_transpose, 0), "pt1": (p_transpose, 1), "pc": (p_copy,), "pq": (p_quant,),
            "oD": (out_diff,), "oO": (out_one,), "cD": (diff_copy,), "cO": (one_copy,), "gm": (gate_mult,), "gs": (gate_sub,),
        }
        order = [("mx0", 3), ("cO", 8), ("pt0", 5), ("sc1", 3), ("pq", 6), ("qq", 2), ("xT", 0), ("gf", 3), ("nm0", 3), ("cD", 7), ("rc", 4), ("qm0", 1), ("ex0", 3), ("gs", 8), ("xc", 0), ("gm", 7), ("mx1", 3), ("gt", 2), ("ga", 2), ("pm1", 4), ("nm1", 3), ("oO", 7), ("sc0", 2), ("pm0", 4), ("qm1", 0), ("oD", 6), ("pc", 5), ("pt1", 4), ("ex1", 3)]
        period = {"xT": (2, 0), "xc": (2, 0), "qm0": (2, 0), "qm1": (2, 0), "qq": (2, 0), "ga": (4, 3), "gf": (4, 3)}
        prologue = {0: (k_transpose,), 1: (k_quant,), 2: (v_widen,), 3: (v_interleave, 0), 4: (v_interleave, 1), 5: (v_quant,)}
        for n in range(NT + max(lag for name, lag in order)):
            for name, lag in order:
                if 0 <= n - lag < NT and (n - lag) % period.get(name, (1, 0))[0] == period.get(name, (1, 0))[1]:
                    stages[name][0](n - lag, *stages[name][1:])
            if n in prologue:
                prologue[n][0](*prologue[n][1:])
